import numpy as np
import ml_dtypes


def mxq(x, axis, fmt="e4m3"):
    dtype, down = {"e4m3": (ml_dtypes.float8_e4m3fn, 7), "e5m2": (ml_dtypes.float8_e5m2, 14)}[fmt]
    v = np.moveaxis(np.asarray(x, np.float32).astype(ml_dtypes.bfloat16).astype(np.float64), axis, -1)
    blocks = v.reshape(v.shape[:-1] + (-1, 32))
    amax = np.abs(blocks).max(-1, keepdims=True)
    byte = np.maximum(np.where(amax > 0, np.frexp(amax)[1] - 1 + 127, 0) - down, 1)
    scale = np.exp2(byte - 127.0)
    codes = (blocks / scale).astype(np.float32).astype(dtype).astype(np.float64)
    return np.moveaxis((codes * scale).reshape(v.shape), -1, axis)


WIDE = False


def mx_kscale(k):
    if not WIDE:
        return np.ones(k)
    levels = np.array([10, -10, 5, -5, 0])
    if k % 512:
        return np.exp2(np.random.permutation(np.resize(levels, k // 32))).repeat(32)
    a = np.empty((k // 512, 16))
    for p in range(k // 512):
        a[p, :8] = np.random.permutation(np.resize(levels, 8))
        for g in range(8):
            far = levels[np.abs(levels - a[p, g]) >= 10]
            a[p, g + 8] = far[np.random.randint(len(far))]
    return np.exp2(a.ravel()).repeat(32)


def f64(x):
    return np.asarray(x).astype(np.float64)


def striped8(idx):
    return np.asarray(idx).reshape(8, -1, 16).transpose(0, 2, 1).reshape(128, -1).astype(np.uint16)


def unstriped8(offs):
    return offs.reshape(8, 16, -1).transpose(0, 2, 1).reshape(8, -1).astype(np.int64)


def pick8(x, idx, run):
    r = np.arange(len(x))
    return x[r[:, None], idx[r % (8 * run) // run]]


E2M1 = np.array([0.0, 0.5, 1.0, 1.5, 2.0, 3.0, 4.0, 6.0, -0.0, -0.5, -1.0, -1.5, -2.0, -3.0, -4.0, -6.0])


def pack_weight(w, fmt):
    k, n = w.shape
    w = f64(np.asarray(w, np.float32).astype(ml_dtypes.bfloat16)).reshape(k // 32, 32, n)
    amax = np.abs(w).max(1)
    if fmt == "e4m3":
        byte = np.frexp(amax)[1] - 1 + 127 - 7
    else:
        mant, ex = np.frexp(amax / 6.0)
        byte = np.where(mant > 0.5, ex, ex - 1) + 127
    byte = np.clip(np.where(amax > 0, byte, 1), 1, 254)
    scaled = (w * np.exp2(127.0 - byte)[:, None, :]).reshape(k, n).astype(np.float32)
    by_word = np.ascontiguousarray(scaled.reshape(k // 512, 128, 4, n).transpose(0, 1, 3, 2))
    if fmt == "e4m3":
        words = by_word.astype(ml_dtypes.float8_e4m3fn).view(np.uint8)
    else:
        c = by_word.astype(ml_dtypes.float4_e2m1fn).view(np.uint8) & 0xF
        words = (c[..., 0::2] | (c[..., 1::2] << 4)).reshape(k // 512, 128, 2 * n)
    return np.ascontiguousarray(words), np.ascontiguousarray(byte.astype(np.uint8).reshape(k // 512, 16, n))


def unpack_weight(words, scales, fmt):
    g, _, n = scales.shape
    words = np.ascontiguousarray(words).reshape(g, 128, n, -1)
    if fmt == "e4m3":
        vals = words.view(ml_dtypes.float8_e4m3fn).astype(np.float64)
    else:
        nib = np.empty((g, 128, n, 4), np.uint8)
        nib[..., 0::2] = words & 0xF
        nib[..., 1::2] = words >> 4
        vals = E2M1[nib]
    vals = vals * np.repeat(np.exp2(scales.astype(np.float64) - 127.0), 8, axis=1)[..., None]
    return vals.transpose(0, 1, 3, 2).reshape(g * 512, n)


D, V, Q, I = 512, 2048, 128, 512


def setup_inputs():
    n = np.random.standard_normal
    idx = np.stack([np.random.permutation(V)[:I] for _ in range(8)])
    fd = mx_kscale(D)
    vocp = pack_weight(n((D, V)) / fd[:, None], "e4m3")
    return {
        "hid": (n((D, Q)) * 1.0 / np.sqrt(D) * fd[:, None]).astype(np.float32),
        "voc_words": vocp[0],
        "voc_scales": vocp[1],
        "th": (np.random.uniform(0.0003, 0.001, (Q, 1))).astype(np.float32),
        "sw": (np.random.uniform(0.5, 2.0, (1, I))).astype(np.float32),
        "dhid": (n((D, Q)) * 1.0 / np.sqrt(D) * fd[:, None]).astype(np.float32),
        "base": (0.5 * n((Q, V))).astype(np.float32),
        "offs": striped8(idx),
    }


def reference(hid, voc_words, voc_scales, th, sw, dhid, base, offs):
    idx = unstriped8(offs)
    vocu = unpack_weight(voc_words, voc_scales, "e4m3")
    hidq = mxq(f64(hid), 0, "e4m3")
    a = hidq.T @ vocu
    dhidq = mxq(f64(dhid), 0, "e4m3")
    ta = dhidq.T @ vocu
    m1 = np.max(a, axis=1, keepdims=True)
    p = np.exp(a - m1)
    z = np.sum(p, axis=1, keepdims=True)
    px = np.exp(pick8(a, idx, 16) - m1)
    dpx = f64(sw) / (px + z * f64(th)) - f64(sw) * px / np.square(px + z * f64(th))
    dz = np.sum(f64(sw) * px / np.square(px + z * f64(th)) * (-1.0), axis=1, keepdims=True) * f64(th)
    xp = ta * p
    xz = np.sum(xp, axis=1, keepdims=True)
    xpx = pick8(ta, idx, 16) * px
    xdpx = (xpx + xz * f64(th)) * f64(sw) / np.square(px + z * f64(th)) * (-1.0) - (xpx * f64(sw) - (xpx + xz * f64(th)) * (px + z * f64(th)) * 2.0 * f64(sw) * px / np.square(px + z * f64(th))) / np.square(px + z * f64(th))
    xdz = np.sum((xpx * f64(sw) - (xpx + xz * f64(th)) * (px + z * f64(th)) * 2.0 * f64(sw) * px / np.square(px + z * f64(th))) / np.square(px + z * f64(th)) * (-1.0), axis=1, keepdims=True) * f64(th)
    xe1 = xdpx * px + xpx * dpx
    xs1 = np.zeros((Q, V))
    xs1[np.arange(Q)[:, None], idx[np.arange(Q) % 128 // 16]] = xe1
    xda = xdz * p + xp * dz + xs1
    y = xda * 2.0 + f64(base)
    return y

@@ -1,0 +1,302 @@
+import math
+from contextlib import ExitStack
+
+import concourse.mybir as mybir
+from concourse.masks import make_identity
+
+F32 = mybir.dt.float32
+BF16 = mybir.dt.bfloat16
+I32 = mybir.dt.int32
+U32 = mybir.dt.uint32
+U16 = mybir.dt.uint16
+U8 = mybir.dt.uint8
+FP8X4 = mybir.dt.float8_e4m3fn_x4
+ALU = mybir.AluOpType
+ACT = mybir.ActivationFunctionType
+AXIS = mybir.AxisListType
+
+P = 128
+PACK = 4
+D, V, Q, SLOTS = 512, 2048, 128, 512
+BANK = 512
+CHUNKS = V // BANK
+FLOPS = 2 * 2 * D * Q * V
+VOC_LOADS = ((0, 512), (512, 1024), (1024, 2048))
+TURNED = (1, 2, 3)
+SHIFT = 191.0 / 648.0
+LINEAR = 10.0 / 27.0
+LOG_PER_BIT = math.log(2.0) / 2.0**23
+
+
+def tile_attend_hvpresence_heads_kernel(tc, hid, voc_words, voc_scales, th, sw, dhid, base, offs, out):
+    nc = tc.nc
+    with ExitStack() as ctx:
+        sb = ctx.enter_context(tc.tile_pool(name="sb", bufs=1))
+        ps = ctx.enter_context(tc.psum_pool(name="ps", bufs=1))
+
+        def column(name, width=1):
+            return sb.tile([P, width], F32, name=name)
+
+        def cols(c):
+            return slice(c * BANK, (c + 1) * BANK)
+
+        offsets = sb.tile([P, SLOTS // 16], U16, name="offsets")
+        hid_raw = sb.tile([P, PACK, Q], F32, name="hid_raw")
+        dhid_raw = sb.tile([P, PACK, Q], F32, name="dhid_raw")
+        voc_parts = [sb.tile([P, hi - lo], U32, name="voc%d" % lo, align_bytes=64) for lo, hi in VOC_LOADS]
+        voc_planes = sb.tile([P, BANK], U8, name="voc_planes", align_bytes=64)
+        th_col = column("th_col")
+        sw_rows = sb.tile([P, SLOTS], F32, name="sw_rows")
+        base_sb = sb.tile([P, V], F32, name="base_sb")
+        xs = sb.tile([P, V], F32, name="xs")
+
+        nc.sync.dma_start(out=hid_raw[:], in_=hid.rearrange("(p j) q -> p j q", j=PACK))
+        nc.vector.memset(voc_planes[:].bitcast(U32), 0)
+        scale_words = voc_scales[0].bitcast(I32)
+        for quad in range(4):
+            nc.sync.dma_start(
+                out=voc_planes[32 * quad : 32 * quad + 16, :].bitcast(I32),
+                in_=scale_words[4 * quad : 4 * quad + 4, :].rearrange("j (c n) -> c j n", c=CHUNKS),
+            )
+        words = voc_words[0].rearrange("p n t -> p (n t)").bitcast(I32)
+        for part, (lo, hi) in zip(voc_parts, VOC_LOADS):
+            nc.sync.dma_start(out=part[:].bitcast(I32), in_=words[:, lo:hi])
+        nc.sync.dma_start(out=dhid_raw[:], in_=dhid.rearrange("(p j) q -> p j q", j=PACK))
+        nc.sync.dma_start(offsets[:], offs)
+        nc.sync.dma_start(out=th_col[:], in_=th)
+        nc.sync.dma_start(out=sw_rows[:], in_=sw[0].partition_broadcast(P))
+        nc.sync.dma_start(out=base_sb[:], in_=base)
+
+        plus6 = column("plus6")
+        nc.vector.memset(plus6[:], 6.0)
+        exp_const, guess_const, square_const = column("exp_const"), column("guess_const"), column("square_const")
+        nc.scalar.activation(out=exp_const[:], in_=plus6[:], func=ACT.Copy, scale=(176.0 - math.log(2.0)) / 6.0)
+        nc.scalar.activation(out=guess_const[:], in_=plus6[:], func=ACT.Copy, scale=(88.5 + SHIFT) / 6.0)
+        nc.scalar.activation(out=square_const[:], in_=plus6[:], func=ACT.Copy, scale=40.0 / 81.0 / 6.0)
+        nc.vector.memset(xs[:], 0.0)
+        identity = sb.tile([P, P], F32, name="identity")
+        make_identity(nc, identity[:])
+
+        def grouped_views(name, raw):
+            grouped = sb.tile([P, Q, PACK], BF16, name=name, align_bytes=64)
+            return (
+                grouped,
+                grouped[:].rearrange("p (c i) t -> p c t i", i=4),
+                raw[:].rearrange("p t (c i) -> p c t i", i=4),
+            )
+
+        def quantise(name, grouped):
+            codes = sb.tile([P, Q], U32, name=name + "_codes", align_bytes=64)
+            scales = sb.tile([P, Q], U8, name=name + "_scales", align_bytes=64)
+            nc.vector.quantize_mx(
+                out=codes[:].bitcast(FP8X4), scales=scales[:], in_=grouped[:].rearrange("p q t -> p (q t)")
+            )
+            return codes, scales
+
+        def scores(bank, c, codes, scales):
+            part = min(c, 2)
+            nc.tensor.matmul_mx(
+                out=bank[:],
+                lhsT=codes[:].bitcast(FP8X4),
+                lhsT_scale=scales[:],
+                rhs=voc_parts[part][:, cols(c - part)].bitcast(FP8X4),
+                rhs_scale=voc_planes[4 * c :, :],
+                start=True,
+                stop=True,
+            )
+
+        hid_grouped, dst, src = grouped_views("hid_grouped", hid_raw)
+        nc.vector.tensor_copy(out=dst, in_=src)
+        hid_codes, hid_scales = quantise("hid", hid_grouped)
+        dhid_grouped, dst, src = grouped_views("dhid_grouped", dhid_raw)
+        nc.scalar.copy(out=dst, in_=src)
+        th_bits = th_col[:].bitcast(U32)
+        exp_bias, guess_bias = column("exp_bias"), column("guess_bias")
+        neg_th = column("neg_th")
+        nc.scalar.activation(out=exp_bias[:], in_=th_bits, func=ACT.Identity, scale=-LOG_PER_BIT, bias=exp_const[:])
+        nc.scalar.activation(out=guess_bias[:], in_=th_bits, func=ACT.Identity, scale=-0.5 * LOG_PER_BIT, bias=guess_const[:])
+        nc.scalar.activation(out=neg_th[:], in_=th_col[:], func=ACT.Copy, scale=-1.0)
+
+        a_banks = [ps.tile([P, BANK], F32, name="a_bank%d" % c) for c in range(CHUNKS)]
+        ta_banks = [ps.tile([P, BANK], F32, name="ta_bank%d" % c) for c in range(CHUNKS)]
+        a_sb = sb.tile([P, V], F32, name="a_sb")
+        ta_sb = sb.tile([P, V], F32, name="ta_sb")
+        chunk_max = column("chunk_max", CHUNKS)
+
+        def copy_a(c):
+            nc.vector.tensor_scalar(
+                out=a_sb[:, cols(c)], in0=a_banks[c][:], scalar1=1.0, scalar2=None,
+                op0=ALU.mult, op1=ALU.max, accum_out=chunk_max[:, c : c + 1],
+            )
+
+        for c in range(CHUNKS):
+            scores(a_banks[c], c, hid_codes, hid_scales)
+        for c in range(CHUNKS):
+            copy_a(c)
+
+        neg_max = column("neg_max")
+        nc.vector.tensor_reduce(out=neg_max[:], in_=chunk_max[:], axis=AXIS.X, op=ALU.max, negate=True)
+        dhid_codes, dhid_scales = quantise("dhid", dhid_grouped)
+        for c in range(CHUNKS):
+            scores(ta_banks[c], c, dhid_codes, dhid_scales)
+
+        ax = sb.tile([P, SLOTS], F32, name="ax")
+        nc.vector.tensor_copy(out=ax[:], in_=a_sb[:].indirect(offsets[:]))
+        p = sb.tile([P, V], F32, name="p")
+        z = column("z")
+        first = slice(0, V // 2)
+        nc.scalar.activation(out=p[:], in_=a_sb[:], func=ACT.Exp, bias=neg_max[:], accum_out=z[:])
+        n0_bias, e1_bias = column("n0_bias"), column("e1_bias")
+        nc.vector.tensor_scalar(
+            out=n0_bias[:], in0=neg_max[:], scalar1=0.5, scalar2=guess_bias[:], op0=ALU.mult, op1=ALU.add
+        )
+        nc.vector.tensor_scalar(
+            out=e1_bias[:], in0=neg_max[:], scalar1=-1.0, scalar2=math.log(LINEAR) - 2.0 * SHIFT,
+            op0=ALU.mult, op1=ALU.add,
+        )
+        for c in (0, 1):
+            nc.vector.tensor_copy(out=ta_sb[:, cols(c)], in_=ta_banks[c][:])
+
+        def turn(bank, source, c, start=False, stop=False):
+            for b in range(4):
+                nc.tensor.matmul(
+                    out=bank[:, b * P : (b + 1) * P],
+                    lhsT=source[:, c * BANK + b * P : c * BANK + (b + 1) * P],
+                    rhs=identity[:],
+                    is_transpose=True,
+                    start=start and b == 0,
+                    stop=stop and b == 3,
+                )
+
+        for c in TURNED:
+            turn(a_banks[c], base_sb, c, start=True)
+
+        def copy_ta_piece(c, lo, hi):
+            nc.scalar.copy(out=ta_sb[:, c * BANK + lo * P : c * BANK + hi * P], in_=ta_banks[c][:, lo * P : hi * P])
+
+        xp = sb.tile([P, V], F32, name="xp")
+        xz_parts = column("xz_parts", 3)
+
+        def make_xp(i, part, ta_part):
+            nc.vector.scalar_tensor_tensor(
+                out=xp[:, part], in0=ta_part, scalar=1.0, in1=p[:, part],
+                op0=ALU.mult, op1=ALU.mult, accum_out=xz_parts[:, i : i + 1],
+            )
+
+        make_xp(0, cols(2), ta_banks[2][:])
+        rz = column("rz")
+        nc.vector.reciprocal(out=rz[:], in_=z[:])
+        make_xp(1, first, ta_sb[:, first])
+
+        neg_zt, e0, n0, n1, e1, n2, g1, g2, tanh_bias = (
+            column(n) for n in ("neg_zt", "e0", "n0", "n1", "e1", "n2", "g1", "g2", "tanh_bias")
+        )
+        copy_ta_piece(3, 0, 1)
+        z_bits = z[:].bitcast(U32)
+        nc.scalar.activation(out=e0[:], in_=z_bits, func=ACT.Exp, scale=-LOG_PER_BIT, bias=exp_bias[:])
+        nc.scalar.activation(out=n0[:], in_=z_bits, func=ACT.Identity, scale=-0.5 * LOG_PER_BIT, bias=n0_bias[:])
+        nc.scalar.activation(out=neg_zt[:], in_=z[:], func=ACT.Copy, scale=neg_th[:])
+        copy_ta_piece(3, 1, 2)
+        nc.scalar.activation(out=n1[:], in_=e0[:], func=ACT.Identity, scale=neg_zt[:], bias=n0[:])
+        copy_ta_piece(3, 2, 4)
+        nc.scalar.activation(out=e1[:], in_=n1[:], func=ACT.Exp, scale=2.0, bias=e1_bias[:])
+        copy_ta_piece(2, 0, 2)
+        nc.scalar.activation(out=g1[:], in_=e1[:], func=ACT.Square, scale=neg_zt[:], bias=square_const[:])
+        nc.scalar.activation(out=n2[:], in_=e1[:], func=ACT.Identity, scale=neg_zt[:], bias=n1[:])
+        copy_ta_piece(2, 2, 3)
+        nc.scalar.activation(out=g2[:], in_=g1[:], func=ACT.Square, scale=9.0 / LINEAR**2, bias=plus6[:])
+        copy_ta_piece(2, 3, 4)
+        nc.scalar.activation(out=tanh_bias[:], in_=g2[:], func=ACT.Identity, scale=1.0 / 648.0, bias=n2[:])
+        t = sb.tile([P, SLOTS], F32, name="t")
+        t2 = sb.tile([P, SLOTS], F32, name="t2")
+        halves = (slice(0, SLOTS // 2), slice(SLOTS // 2, SLOTS))
+        for half in halves:
+            nc.scalar.activation(out=t[:, half], in_=ax[:, half], func=ACT.Tanh, scale=0.5, bias=tanh_bias[:])
+        for half in halves:
+            nc.scalar.activation(out=t2[:, half], in_=t[:, half], func=ACT.Square)
+
+        make_xp(2, cols(3), ta_sb[:, cols(3)])
+        tx = sb.tile([P, SLOTS], F32, name="tx")
+        nc.vector.tensor_copy(out=tx[:], in_=ta_sb[:].indirect(offsets[:]))
+        mean_parts = column("mean_parts", 3)
+        neg_mean = column("neg_mean")
+        nc.vector.tensor_scalar(
+            out=mean_parts[:], in0=xz_parts[:], scalar1=rz[:], scalar2=None,
+            op0=ALU.mult, op1=ALU.subtract, accum_out=neg_mean[:],
+        )
+
+        half_rz, minus2_rz = column("half_rz"), column("minus2_rz")
+        nc.scalar.activation(out=half_rz[:], in_=rz[:], func=ACT.Copy, scale=0.5)
+        nc.scalar.activation(out=minus2_rz[:], in_=rz[:], func=ACT.Copy, scale=-2.0)
+
+        h = sb.tile([P, SLOTS], F32, name="h")
+        neg_w = sb.tile([P, SLOTS], F32, name="neg_w")
+        xe1 = sb.tile([P, SLOTS], F32, name="xe1")
+        neg_w_sum, xe1_sum = column("neg_w_sum"), column("xe1_sum")
+        beta, neg_beta_mean, alpha = column("beta"), column("neg_beta_mean"), column("alpha")
+        acc1 = sb.tile([P, V], F32, name="acc1")
+
+        def add_xp(lo, hi):
+            nc.vector.scalar_tensor_tensor(
+                out=acc1[:, lo:hi], in0=xp[:, lo:hi], scalar=beta[:], in1=base_sb[:, lo:hi], op0=ALU.mult, op1=ALU.add
+            )
+
+        nc.vector.scalar_tensor_tensor(
+            out=neg_w[:], in0=t2[:], scalar=-1.0, in1=sw_rows[:], op0=ALU.add, op1=ALU.mult,
+            accum_out=neg_w_sum[:],
+        )
+        nc.scalar.activation(out=beta[:], in_=neg_w_sum[:], func=ACT.Copy, scale=half_rz[:])
+        nc.vector.scalar_tensor_tensor(
+            out=h[:], in0=tx[:], scalar=neg_mean[:], in1=t[:], op0=ALU.add, op1=ALU.mult
+        )
+        add_xp(0, BANK // 2)
+        nc.vector.scalar_tensor_tensor(
+            out=xe1[:], in0=h[:], scalar=0.25, in1=neg_w[:], op0=ALU.mult, op1=ALU.mult,
+            accum_out=xe1_sum[:],
+        )
+        add_xp(BANK // 2, BANK)
+        nc.vector.tensor_copy(out=xs[:].indirect(offsets[:]), in_=xe1[:])
+
+        xp_term = sb.tile([P, V], F32, name="xp_term")
+        p_term = sb.tile([P, V], F32, name="p_term")
+        turned_sum = sb.tile([P, V], F32, name="turned_sum")
+
+        def scale_xp(c):
+            nc.scalar.activation(out=xp_term[:, cols(c)], in_=xp[:, cols(c)], func=ACT.Copy, scale=beta[:])
+            turn(a_banks[c], xp_term, c)
+
+        def scale_p(c):
+            nc.scalar.activation(out=p_term[:, cols(c)], in_=p[:, cols(c)], func=ACT.Copy, scale=alpha[:])
+            turn(a_banks[c], p_term, c, stop=True)
+
+        def turn_back(c):
+            nc.scalar.copy(out=turned_sum[:, cols(c)], in_=a_banks[c][:])
+            turn(ta_banks[c], turned_sum, c, start=True, stop=True)
+
+        scale_xp(TURNED[0])
+        nc.scalar.activation(out=neg_beta_mean[:], in_=beta[:], func=ACT.Copy, scale=neg_mean[:])
+        scale_xp(TURNED[1])
+        nc.scalar.activation(out=alpha[:], in_=xe1_sum[:], func=ACT.Identity, scale=minus2_rz[:], bias=neg_beta_mean[:])
+        scale_xp(TURNED[2])
+        scale_p(TURNED[0])
+        for before, c in zip(TURNED, TURNED[1:]):
+            scale_p(c)
+            turn_back(before)
+        turn_back(TURNED[-1])
+
+        acc2 = sb.tile([P, V], F32, name="acc2")
+        result = [sb.tile([P, BANK], F32, name="result%d" % c) for c in range(CHUNKS)]
+
+        def finish(c, dense):
+            nc.vector.scalar_tensor_tensor(
+                out=result[c][:], in0=xs[:, cols(c)], scalar=2.0, in1=dense, op0=ALU.mult, op1=ALU.add
+            )
+            nc.sync.dma_start(out=out[:, cols(c)], in_=result[c][:])
+
+        nc.vector.scalar_tensor_tensor(
+            out=acc2[:, cols(0)], in0=p[:, cols(0)], scalar=alpha[:], in1=acc1[:, cols(0)], op0=ALU.mult, op1=ALU.add
+        )
+        finish(1, ta_banks[1][:])
+        finish(0, acc2[:, cols(0)])
+        finish(2, ta_banks[2][:])
+        finish(3, ta_banks[3][:])

@@ -22,7 +22,8 @@ BANK = 512
 CHUNKS = V // BANK
 FLOPS = 2 * 2 * D * Q * V
 VOC_LOADS = ((0, 512), (512, 1024), (1024, 2048))
-TURNED = (1, 2, 3)
+DIRECT = 640
+LAST_STORE = 256
 SHIFT = 191.0 / 648.0
 LINEAR = 10.0 / 27.0
 LOG_PER_BIT = math.log(2.0) / 2.0**23
@@ -54,7 +55,7 @@ def tile_attend_hvpresence_heads_kernel(tc, hid, voc_words, voc_scales, th, sw, 
         nc.vector.memset(voc_planes[:].bitcast(U32), 0)
         scale_words = voc_scales[0].bitcast(I32)
         for quad in range(4):
-            nc.sync.dma_start(
+            nc.scalar.dma_start(
                 out=voc_planes[32 * quad : 32 * quad + 16, :].bitcast(I32),
                 in_=scale_words[4 * quad : 4 * quad + 4, :].rearrange("j (c n) -> c j n", c=CHUNKS),
             )
@@ -63,7 +64,7 @@ def tile_attend_hvpresence_heads_kernel(tc, hid, voc_words, voc_scales, th, sw, 
             nc.sync.dma_start(out=part[:].bitcast(I32), in_=words[:, lo:hi])
         nc.sync.dma_start(out=dhid_raw[:], in_=dhid.rearrange("(p j) q -> p j q", j=PACK))
         nc.sync.dma_start(offsets[:], offs)
-        nc.sync.dma_start(out=th_col[:], in_=th)
+        nc.gpsimd.dma_start(out=th_col[:], in_=th)
         nc.sync.dma_start(out=sw_rows[:], in_=sw[0].partition_broadcast(P))
         nc.sync.dma_start(out=base_sb[:], in_=base)
 
@@ -72,7 +73,12 @@ def tile_attend_hvpresence_heads_kernel(tc, hid, voc_words, voc_scales, th, sw, 
         exp_const, guess_const, square_const = column("exp_const"), column("guess_const"), column("square_const")
         nc.scalar.activation(out=exp_const[:], in_=plus6[:], func=ACT.Copy, scale=(176.0 - math.log(2.0)) / 6.0)
         nc.scalar.activation(out=guess_const[:], in_=plus6[:], func=ACT.Copy, scale=(88.5 + SHIFT) / 6.0)
+        e1_const = column("e1_const")
+        nc.scalar.activation(out=e1_const[:], in_=plus6[:], func=ACT.Copy, scale=(math.log(LINEAR) - 2.0 * SHIFT) / 6.0)
         nc.scalar.activation(out=square_const[:], in_=plus6[:], func=ACT.Copy, scale=40.0 / 81.0 / 6.0)
+        rz_factors = column("rz_factors", 2)
+        for i, factor in enumerate((0.5, -2.0)):
+            nc.vector.memset(rz_factors[:, i : i + 1], factor)
         nc.vector.memset(xs[:], 0.0)
         identity = sb.tile([P, P], F32, name="identity")
         make_identity(nc, identity[:])
@@ -144,32 +150,25 @@ def tile_attend_hvpresence_heads_kernel(tc, hid, voc_words, voc_scales, th, sw, 
         nc.vector.tensor_copy(out=ax[:], in_=a_sb[:].indirect(offsets[:]))
         p = sb.tile([P, V], F32, name="p")
         z = column("z")
-        first = slice(0, V // 2)
         nc.scalar.activation(out=p[:], in_=a_sb[:], func=ACT.Exp, bias=neg_max[:], accum_out=z[:])
-        n0_bias, e1_bias = column("n0_bias"), column("e1_bias")
-        nc.vector.tensor_scalar(
-            out=n0_bias[:], in0=neg_max[:], scalar1=0.5, scalar2=guess_bias[:], op0=ALU.mult, op1=ALU.add
-        )
-        nc.vector.tensor_scalar(
-            out=e1_bias[:], in0=neg_max[:], scalar1=-1.0, scalar2=math.log(LINEAR) - 2.0 * SHIFT,
-            op0=ALU.mult, op1=ALU.add,
-        )
         for c in (0, 1):
             nc.vector.tensor_copy(out=ta_sb[:, cols(c)], in_=ta_banks[c][:])
 
-        def turn(bank, source, c, start=False, stop=False):
-            for b in range(4):
+        turned = [(c, max(c * BANK, DIRECT), (c + 1) * BANK) for c in range(DIRECT // BANK, CHUNKS)]
+
+        def turn(bank, source, lo, hi, start=False, stop=False):
+            for at in range(lo, hi, P):
                 nc.tensor.matmul(
-                    out=bank[:, b * P : (b + 1) * P],
-                    lhsT=source[:, c * BANK + b * P : c * BANK + (b + 1) * P],
+                    out=bank[:, at - lo : at - lo + P],
+                    lhsT=source[:, at : at + P],
                     rhs=identity[:],
                     is_transpose=True,
-                    start=start and b == 0,
-                    stop=stop and b == 3,
+                    start=start and at == lo,
+                    stop=stop and at == hi - P,
                 )
 
-        for c in TURNED:
-            turn(a_banks[c], base_sb, c, start=True)
+        for c, lo, hi in turned:
+            turn(a_banks[c], base_sb, lo, hi, start=True)
 
         def copy_ta_piece(c, lo, hi):
             nc.scalar.copy(out=ta_sb[:, c * BANK + lo * P : c * BANK + hi * P], in_=ta_banks[c][:, lo * P : hi * P])
@@ -186,23 +185,24 @@ def tile_attend_hvpresence_heads_kernel(tc, hid, voc_words, voc_scales, th, sw, 
         make_xp(0, cols(2), ta_banks[2][:])
         rz = column("rz")
         nc.vector.reciprocal(out=rz[:], in_=z[:])
-        make_xp(1, first, ta_sb[:, first])
+        make_xp(1, slice(0, 2 * BANK), ta_sb[:, : 2 * BANK])
 
-        neg_zt, e0, n0, n1, e1, n2, g1, g2, tanh_bias = (
-            column(n) for n in ("neg_zt", "e0", "n0", "n1", "e1", "n2", "g1", "g2", "tanh_bias")
+        neg_zt, e0, n0, n1, e1, n1m, n2, g1, g2, tanh_bias = (
+            column(n) for n in ("neg_zt", "e0", "n0", "n1", "e1", "n1m", "n2", "g1", "g2", "tanh_bias")
         )
         copy_ta_piece(3, 0, 1)
         z_bits = z[:].bitcast(U32)
         nc.scalar.activation(out=e0[:], in_=z_bits, func=ACT.Exp, scale=-LOG_PER_BIT, bias=exp_bias[:])
-        nc.scalar.activation(out=n0[:], in_=z_bits, func=ACT.Identity, scale=-0.5 * LOG_PER_BIT, bias=n0_bias[:])
+        nc.scalar.activation(out=n0[:], in_=z_bits, func=ACT.Identity, scale=-0.5 * LOG_PER_BIT, bias=guess_bias[:])
         nc.scalar.activation(out=neg_zt[:], in_=z[:], func=ACT.Copy, scale=neg_th[:])
         copy_ta_piece(3, 1, 2)
         nc.scalar.activation(out=n1[:], in_=e0[:], func=ACT.Identity, scale=neg_zt[:], bias=n0[:])
         copy_ta_piece(3, 2, 4)
-        nc.scalar.activation(out=e1[:], in_=n1[:], func=ACT.Exp, scale=2.0, bias=e1_bias[:])
+        nc.scalar.activation(out=e1[:], in_=n1[:], func=ACT.Exp, scale=2.0, bias=e1_const[:])
+        nc.scalar.activation(out=n1m[:], in_=neg_max[:], func=ACT.Identity, scale=0.5, bias=n1[:])
         copy_ta_piece(2, 0, 2)
         nc.scalar.activation(out=g1[:], in_=e1[:], func=ACT.Square, scale=neg_zt[:], bias=square_const[:])
-        nc.scalar.activation(out=n2[:], in_=e1[:], func=ACT.Identity, scale=neg_zt[:], bias=n1[:])
+        nc.scalar.activation(out=n2[:], in_=e1[:], func=ACT.Identity, scale=neg_zt[:], bias=n1m[:])
         copy_ta_piece(2, 2, 3)
         nc.scalar.activation(out=g2[:], in_=g1[:], func=ACT.Square, scale=9.0 / LINEAR**2, bias=plus6[:])
         copy_ta_piece(2, 3, 4)
@@ -216,6 +216,9 @@ def tile_attend_hvpresence_heads_kernel(tc, hid, voc_words, voc_scales, th, sw, 
             nc.scalar.activation(out=t2[:, half], in_=t[:, half], func=ACT.Square)
 
         make_xp(2, cols(3), ta_sb[:, cols(3)])
+        rz_times = column("rz_times", 2)
+        half_rz, minus2_rz = rz_times[:, 0:1], rz_times[:, 1:2]
+        nc.scalar.activation(out=rz_times[:], in_=rz_factors[:], func=ACT.Copy, scale=rz[:])
         tx = sb.tile([P, SLOTS], F32, name="tx")
         nc.vector.tensor_copy(out=tx[:], in_=ta_sb[:].indirect(offsets[:]))
         mean_parts = column("mean_parts", 3)
@@ -225,16 +228,13 @@ def tile_attend_hvpresence_heads_kernel(tc, hid, voc_words, voc_scales, th, sw, 
             op0=ALU.mult, op1=ALU.subtract, accum_out=neg_mean[:],
         )
 
-        half_rz, minus2_rz = column("half_rz"), column("minus2_rz")
-        nc.scalar.activation(out=half_rz[:], in_=rz[:], func=ACT.Copy, scale=0.5)
-        nc.scalar.activation(out=minus2_rz[:], in_=rz[:], func=ACT.Copy, scale=-2.0)
-
         h = sb.tile([P, SLOTS], F32, name="h")
         neg_w = sb.tile([P, SLOTS], F32, name="neg_w")
         xe1 = sb.tile([P, SLOTS], F32, name="xe1")
         neg_w_sum, xe1_sum = column("neg_w_sum"), column("xe1_sum")
         beta, neg_beta_mean, alpha = column("beta"), column("neg_beta_mean"), column("alpha")
-        acc1 = sb.tile([P, V], F32, name="acc1")
+        acc1 = sb.tile([P, DIRECT], F32, name="acc1")
+        acc2 = sb.tile([P, DIRECT], F32, name="acc2")
 
         def add_xp(lo, hi):
             nc.vector.scalar_tensor_tensor(
@@ -245,58 +245,61 @@ def tile_attend_hvpresence_heads_kernel(tc, hid, voc_words, voc_scales, th, sw, 
             out=neg_w[:], in0=t2[:], scalar=-1.0, in1=sw_rows[:], op0=ALU.add, op1=ALU.mult,
             accum_out=neg_w_sum[:],
         )
-        nc.scalar.activation(out=beta[:], in_=neg_w_sum[:], func=ACT.Copy, scale=half_rz[:])
+        nc.scalar.activation(out=beta[:], in_=neg_w_sum[:], func=ACT.Copy, scale=half_rz)
         nc.vector.scalar_tensor_tensor(
             out=h[:], in0=tx[:], scalar=neg_mean[:], in1=t[:], op0=ALU.add, op1=ALU.mult
         )
-        add_xp(0, BANK // 2)
+        add_xp(0, 2 * P)
         nc.vector.scalar_tensor_tensor(
             out=xe1[:], in0=h[:], scalar=0.25, in1=neg_w[:], op0=ALU.mult, op1=ALU.mult,
             accum_out=xe1_sum[:],
         )
-        add_xp(BANK // 2, BANK)
+        add_xp(2 * P, DIRECT)
         nc.vector.tensor_copy(out=xs[:].indirect(offsets[:]), in_=xe1[:])
 
         xp_term = sb.tile([P, V], F32, name="xp_term")
         p_term = sb.tile([P, V], F32, name="p_term")
         turned_sum = sb.tile([P, V], F32, name="turned_sum")
 
-        def scale_xp(c):
-            nc.scalar.activation(out=xp_term[:, cols(c)], in_=xp[:, cols(c)], func=ACT.Copy, scale=beta[:])
-            turn(a_banks[c], xp_term, c)
+        def scale_xp(c, lo, hi):
+            nc.scalar.activation(out=xp_term[:, lo:hi], in_=xp[:, lo:hi], func=ACT.Copy, scale=beta[:])
+            turn(a_banks[c], xp_term, lo, hi)
 
-        def scale_p(c):
-            nc.scalar.activation(out=p_term[:, cols(c)], in_=p[:, cols(c)], func=ACT.Copy, scale=alpha[:])
-            turn(a_banks[c], p_term, c, stop=True)
+        def scale_p(c, lo, hi):
+            nc.scalar.activation(out=p_term[:, lo:hi], in_=p[:, lo:hi], func=ACT.Copy, scale=alpha[:])
+            turn(a_banks[c], p_term, lo, hi, stop=True)
 
-        def turn_back(c):
-            nc.scalar.copy(out=turned_sum[:, cols(c)], in_=a_banks[c][:])
-            turn(ta_banks[c], turned_sum, c, start=True, stop=True)
+        def turn_back(c, lo, hi):
+            nc.scalar.copy(out=turned_sum[:, lo:hi], in_=a_banks[c][:, : hi - lo])
+            turn(ta_banks[c], turned_sum, lo, hi, start=True, stop=True)
 
-        scale_xp(TURNED[0])
+        scale_xp(*turned[0])
         nc.scalar.activation(out=neg_beta_mean[:], in_=beta[:], func=ACT.Copy, scale=neg_mean[:])
-        scale_xp(TURNED[1])
-        nc.scalar.activation(out=alpha[:], in_=xe1_sum[:], func=ACT.Identity, scale=minus2_rz[:], bias=neg_beta_mean[:])
-        scale_xp(TURNED[2])
-        scale_p(TURNED[0])
-        for before, c in zip(TURNED, TURNED[1:]):
-            scale_p(c)
-            turn_back(before)
-        turn_back(TURNED[-1])
+        scale_xp(*turned[1])
+        nc.scalar.activation(out=alpha[:], in_=xe1_sum[:], func=ACT.Identity, scale=minus2_rz, bias=neg_beta_mean[:])
+        scale_xp(*turned[2])
+        scale_p(*turned[0])
+        for before, now in zip(turned, turned[1:]):
+            scale_p(*now)
+            turn_back(*before)
+        turn_back(*turned[-1])
 
-        acc2 = sb.tile([P, V], F32, name="acc2")
-        result = [sb.tile([P, BANK], F32, name="result%d" % c) for c in range(CHUNKS)]
+        result = sb.tile([P, V], F32, name="result")
 
-        def finish(c, dense):
+        def finish(lo, hi, dense):
             nc.vector.scalar_tensor_tensor(
-                out=result[c][:], in0=xs[:, cols(c)], scalar=2.0, in1=dense, op0=ALU.mult, op1=ALU.add
+                out=result[:, lo:hi], in0=xs[:, lo:hi], scalar=2.0, in1=dense, op0=ALU.mult, op1=ALU.add
             )
-            nc.sync.dma_start(out=out[:, cols(c)], in_=result[c][:])
+            nc.sync.dma_start(out=out[:, lo:hi], in_=result[:, lo:hi])
 
+        c, lo, hi = turned[0]
+        finish(lo, hi, ta_banks[c][:, : hi - lo])
         nc.vector.scalar_tensor_tensor(
-            out=acc2[:, cols(0)], in0=p[:, cols(0)], scalar=alpha[:], in1=acc1[:, cols(0)], op0=ALU.mult, op1=ALU.add
+            out=acc2[:], in0=p[:, :DIRECT], scalar=alpha[:], in1=acc1[:], op0=ALU.mult, op1=ALU.add
         )
-        finish(1, ta_banks[1][:])
-        finish(0, acc2[:, cols(0)])
-        finish(2, ta_banks[2][:])
-        finish(3, ta_banks[3][:])
+        c, lo, hi = turned[1]
+        finish(lo, hi, ta_banks[c][:])
+        finish(0, DIRECT, acc2[:])
+        c, lo, hi = turned[2]
+        finish(lo, hi - LAST_STORE, ta_banks[c][:, : BANK - LAST_STORE])
+        finish(hi - LAST_STORE, hi, ta_banks[c][:, BANK - LAST_STORE :])

@@ -22,7 +22,7 @@ BANK = 512
 CHUNKS = V // BANK
 FLOPS = 2 * 2 * D * Q * V
 VOC_LOADS = ((0, 512), (512, 1024), (1024, 2048))
-DIRECT = 640
+DIRECT = 768
 LAST_STORE = 256
 SHIFT = 191.0 / 648.0
 LINEAR = 10.0 / 27.0
@@ -55,7 +55,7 @@ def tile_attend_hvpresence_heads_kernel(tc, hid, voc_words, voc_scales, th, sw, 
         nc.vector.memset(voc_planes[:].bitcast(U32), 0)
         scale_words = voc_scales[0].bitcast(I32)
         for quad in range(4):
-            nc.scalar.dma_start(
+            nc.sync.dma_start(
                 out=voc_planes[32 * quad : 32 * quad + 16, :].bitcast(I32),
                 in_=scale_words[4 * quad : 4 * quad + 4, :].rearrange("j (c n) -> c j n", c=CHUNKS),
             )
@@ -159,7 +159,7 @@ def tile_attend_hvpresence_heads_kernel(tc, hid, voc_words, voc_scales, th, sw, 
         def turn(bank, source, lo, hi, start=False, stop=False):
             for at in range(lo, hi, P):
                 nc.tensor.matmul(
-                    out=bank[:, at - lo : at - lo + P],
+                    out=bank[:, at % BANK : at % BANK + P],
                     lhsT=source[:, at : at + P],
                     rhs=identity[:],
                     is_transpose=True,
@@ -270,19 +270,24 @@ def tile_attend_hvpresence_heads_kernel(tc, hid, voc_words, voc_scales, th, sw, 
             turn(a_banks[c], p_term, lo, hi, stop=True)
 
         def turn_back(c, lo, hi):
-            nc.scalar.copy(out=turned_sum[:, lo:hi], in_=a_banks[c][:, : hi - lo])
+            nc.scalar.copy(out=turned_sum[:, lo:hi], in_=a_banks[c][:, lo % BANK :])
             turn(ta_banks[c], turned_sum, lo, hi, start=True, stop=True)
 
-        scale_xp(*turned[0])
+        c, lo, hi = turned[0]
+        scale_xp(c, lo, lo + P)
+        scale_xp(c, lo + P, hi)
         nc.scalar.activation(out=neg_beta_mean[:], in_=beta[:], func=ACT.Copy, scale=neg_mean[:])
-        scale_xp(*turned[1])
+        for piece in turned[1:]:
+            scale_xp(*piece)
         nc.scalar.activation(out=alpha[:], in_=xe1_sum[:], func=ACT.Identity, scale=minus2_rz, bias=neg_beta_mean[:])
-        scale_xp(*turned[2])
-        scale_p(*turned[0])
-        for before, now in zip(turned, turned[1:]):
-            scale_p(*now)
-            turn_back(*before)
-        turn_back(*turned[-1])
+        nc.gpsimd.tensor_scalar(
+            out=p_term[:, :DIRECT], in0=p[:, :DIRECT], scalar1=alpha[:], scalar2=0.0, op0=ALU.mult, op1=ALU.add
+        )
+        nc.gpsimd.tensor_tensor(out=acc2[:], in0=acc1[:], in1=p_term[:, :DIRECT], op=ALU.add)
+        for piece in turned:
+            scale_p(*piece)
+        for piece in turned:
+            turn_back(*piece)
 
         result = sb.tile([P, V], F32, name="result")
 
@@ -293,10 +298,7 @@ def tile_attend_hvpresence_heads_kernel(tc, hid, voc_words, voc_scales, th, sw, 
             nc.sync.dma_start(out=out[:, lo:hi], in_=result[:, lo:hi])
 
         c, lo, hi = turned[0]
-        finish(lo, hi, ta_banks[c][:, : hi - lo])
-        nc.vector.scalar_tensor_tensor(
-            out=acc2[:], in0=p[:, :DIRECT], scalar=alpha[:], in1=acc1[:], op0=ALU.mult, op1=ALU.add
-        )
+        finish(lo, hi, ta_banks[c][:, lo % BANK :])
         c, lo, hi = turned[1]
         finish(lo, hi, ta_banks[c][:])
         finish(0, DIRECT, acc2[:])

@@ -23,7 +23,7 @@ CHUNKS = V // BANK
 FLOPS = 2 * 2 * D * Q * V
 VOC_LOADS = ((0, 512), (512, 1024), (1024, 2048))
 DIRECT = 768
-LAST_STORE = 256
+LAST_STORE = 128
 SHIFT = 191.0 / 648.0
 LINEAR = 10.0 / 27.0
 LOG_PER_BIT = math.log(2.0) / 2.0**23
@@ -221,12 +221,11 @@ def tile_attend_hvpresence_heads_kernel(tc, hid, voc_words, voc_scales, th, sw, 
         nc.scalar.activation(out=rz_times[:], in_=rz_factors[:], func=ACT.Copy, scale=rz[:])
         tx = sb.tile([P, SLOTS], F32, name="tx")
         nc.vector.tensor_copy(out=tx[:], in_=ta_sb[:].indirect(offsets[:]))
-        mean_parts = column("mean_parts", 3)
-        neg_mean = column("neg_mean")
-        nc.vector.tensor_scalar(
-            out=mean_parts[:], in0=xz_parts[:], scalar1=rz[:], scalar2=None,
-            op0=ALU.mult, op1=ALU.subtract, accum_out=neg_mean[:],
+        xz, neg_mean = column("xz"), column("neg_mean")
+        nc.gpsimd.tensor_scalar(
+            out=xz[:], in0=xz_parts[:, 0:1], scalar1=xz_parts[:, 1:2], scalar2=xz_parts[:, 2:3], op0=ALU.add, op1=ALU.add
         )
+        nc.gpsimd.tensor_scalar(out=neg_mean[:], in0=xz[:], scalar1=rz[:], scalar2=-1.0, op0=ALU.mult, op1=ALU.mult)
 
         h = sb.tile([P, SLOTS], F32, name="h")
         neg_w = sb.tile([P, SLOTS], F32, name="neg_w")
@@ -277,9 +276,13 @@ def tile_attend_hvpresence_heads_kernel(tc, hid, voc_words, voc_scales, th, sw, 
         scale_xp(c, lo, lo + P)
         scale_xp(c, lo + P, hi)
         nc.scalar.activation(out=neg_beta_mean[:], in_=beta[:], func=ACT.Copy, scale=neg_mean[:])
-        for piece in turned[1:]:
-            scale_xp(*piece)
-        nc.scalar.activation(out=alpha[:], in_=xe1_sum[:], func=ACT.Identity, scale=minus2_rz, bias=neg_beta_mean[:])
+        c, lo, hi = turned[1]
+        scale_xp(c, lo, lo + 2 * P)
+        scale_xp(c, lo + 2 * P, hi)
+        scale_xp(*turned[2])
+        nc.gpsimd.tensor_scalar(
+            out=alpha[:], in0=xe1_sum[:], scalar1=minus2_rz, scalar2=neg_beta_mean[:], op0=ALU.mult, op1=ALU.add
+        )
         nc.gpsimd.tensor_scalar(
             out=p_term[:, :DIRECT], in0=p[:, :DIRECT], scalar1=alpha[:], scalar2=0.0, op0=ALU.mult, op1=ALU.add
         )
@@ -297,11 +300,12 @@ def tile_attend_hvpresence_heads_kernel(tc, hid, voc_words, voc_scales, th, sw, 
             )
             nc.sync.dma_start(out=out[:, lo:hi], in_=result[:, lo:hi])
 
+        finish(0, DIRECT // 2, acc2[:, : DIRECT // 2])
+        finish(DIRECT // 2, DIRECT, acc2[:, DIRECT // 2 :])
         c, lo, hi = turned[0]
         finish(lo, hi, ta_banks[c][:, lo % BANK :])
         c, lo, hi = turned[1]
         finish(lo, hi, ta_banks[c][:])
-        finish(0, DIRECT, acc2[:])
         c, lo, hi = turned[2]
         finish(lo, hi - LAST_STORE, ta_banks[c][:, : BANK - LAST_STORE])
         finish(hi - LAST_STORE, hi, ta_banks[c][:, BANK - LAST_STORE :])

import math
from contextlib import ExitStack

import concourse.mybir as mybir
from concourse.masks import make_identity

F32 = mybir.dt.float32
BF16 = mybir.dt.bfloat16
I32 = mybir.dt.int32
U32 = mybir.dt.uint32
U16 = mybir.dt.uint16
U8 = mybir.dt.uint8
FP8X4 = mybir.dt.float8_e4m3fn_x4
ALU = mybir.AluOpType
ACT = mybir.ActivationFunctionType
AXIS = mybir.AxisListType

P = 128
PACK = 4
D, V, Q, SLOTS = 512, 2048, 128, 512
BANK = 512
CHUNKS = V // BANK
FLOPS = 2 * 2 * D * Q * V
VOC_LOADS = ((0, 512), (512, 1024), (1024, 2048))
DIRECT = 768
LAST_STORE = 128
SHIFT = 191.0 / 648.0
LINEAR = 10.0 / 27.0
LOG_PER_BIT = math.log(2.0) / 2.0**23


def tile_attend_hvpresence_heads_kernel(tc, hid, voc_words, voc_scales, th, sw, dhid, base, offs, out):
    nc = tc.nc
    with ExitStack() as ctx:
        sb = ctx.enter_context(tc.tile_pool(name="sb", bufs=1))
        ps = ctx.enter_context(tc.psum_pool(name="ps", bufs=1))

        def column(name, width=1):
            return sb.tile([P, width], F32, name=name)

        def cols(c):
            return slice(c * BANK, (c + 1) * BANK)

        offsets = sb.tile([P, SLOTS // 16], U16, name="offsets")
        hid_raw = sb.tile([P, PACK, Q], F32, name="hid_raw")
        dhid_raw = sb.tile([P, PACK, Q], F32, name="dhid_raw")
        voc_parts = [sb.tile([P, hi - lo], U32, name="voc%d" % lo, align_bytes=64) for lo, hi in VOC_LOADS]
        voc_planes = sb.tile([P, BANK], U8, name="voc_planes", align_bytes=64)
        th_col = column("th_col")
        sw_rows = sb.tile([P, SLOTS], F32, name="sw_rows")
        base_sb = sb.tile([P, V], F32, name="base_sb")
        xs = sb.tile([P, V], F32, name="xs")

        nc.sync.dma_start(out=hid_raw[:], in_=hid.rearrange("(p j) q -> p j q", j=PACK))
        nc.vector.memset(voc_planes[:].bitcast(U32), 0)
        scale_words = voc_scales[0].bitcast(I32)
        for quad in range(4):
            nc.sync.dma_start(
                out=voc_planes[32 * quad : 32 * quad + 16, :].bitcast(I32),
                in_=scale_words[4 * quad : 4 * quad + 4, :].rearrange("j (c n) -> c j n", c=CHUNKS),
            )
        words = voc_words[0].rearrange("p n t -> p (n t)").bitcast(I32)
        for part, (lo, hi) in zip(voc_parts, VOC_LOADS):
            nc.sync.dma_start(out=part[:].bitcast(I32), in_=words[:, lo:hi])
        nc.sync.dma_start(out=dhid_raw[:], in_=dhid.rearrange("(p j) q -> p j q", j=PACK))
        nc.sync.dma_start(offsets[:], offs)
        nc.gpsimd.dma_start(out=th_col[:], in_=th)
        nc.sync.dma_start(out=sw_rows[:], in_=sw[0].partition_broadcast(P))
        nc.sync.dma_start(out=base_sb[:], in_=base)

        plus6 = column("plus6")
        nc.vector.memset(plus6[:], 6.0)
        exp_const, guess_const, square_const = column("exp_const"), column("guess_const"), column("square_const")
        nc.scalar.activation(out=exp_const[:], in_=plus6[:], func=ACT.Copy, scale=(176.0 - math.log(2.0)) / 6.0)
        nc.scalar.activation(out=guess_const[:], in_=plus6[:], func=ACT.Copy, scale=(88.5 + SHIFT) / 6.0)
        e1_const = column("e1_const")
        nc.scalar.activation(out=e1_const[:], in_=plus6[:], func=ACT.Copy, scale=(math.log(LINEAR) - 2.0 * SHIFT) / 6.0)
        nc.scalar.activation(out=square_const[:], in_=plus6[:], func=ACT.Copy, scale=40.0 / 81.0 / 6.0)
        rz_factors = column("rz_factors", 2)
        for i, factor in enumerate((0.5, -2.0)):
            nc.vector.memset(rz_factors[:, i : i + 1], factor)
        nc.vector.memset(xs[:], 0.0)
        identity = sb.tile([P, P], F32, name="identity")
        make_identity(nc, identity[:])

        def grouped_views(name, raw):
            grouped = sb.tile([P, Q, PACK], BF16, name=name, align_bytes=64)
            return (
                grouped,
                grouped[:].rearrange("p (c i) t -> p c t i", i=4),
                raw[:].rearrange("p t (c i) -> p c t i", i=4),
            )

        def quantise(name, grouped):
            codes = sb.tile([P, Q], U32, name=name + "_codes", align_bytes=64)
            scales = sb.tile([P, Q], U8, name=name + "_scales", align_bytes=64)
            nc.vector.quantize_mx(
                out=codes[:].bitcast(FP8X4), scales=scales[:], in_=grouped[:].rearrange("p q t -> p (q t)")
            )
            return codes, scales

        def scores(bank, c, codes, scales):
            part = min(c, 2)
            nc.tensor.matmul_mx(
                out=bank[:],
                lhsT=codes[:].bitcast(FP8X4),
                lhsT_scale=scales[:],
                rhs=voc_parts[part][:, cols(c - part)].bitcast(FP8X4),
                rhs_scale=voc_planes[4 * c :, :],
                start=True,
                stop=True,
            )

        hid_grouped, dst, src = grouped_views("hid_grouped", hid_raw)
        nc.vector.tensor_copy(out=dst, in_=src)
        hid_codes, hid_scales = quantise("hid", hid_grouped)
        dhid_grouped, dst, src = grouped_views("dhid_grouped", dhid_raw)
        nc.scalar.copy(out=dst, in_=src)
        th_bits = th_col[:].bitcast(U32)
        exp_bias, guess_bias = column("exp_bias"), column("guess_bias")
        neg_th = column("neg_th")
        nc.scalar.activation(out=exp_bias[:], in_=th_bits, func=ACT.Identity, scale=-LOG_PER_BIT, bias=exp_const[:])
        nc.scalar.activation(out=guess_bias[:], in_=th_bits, func=ACT.Identity, scale=-0.5 * LOG_PER_BIT, bias=guess_const[:])
        nc.scalar.activation(out=neg_th[:], in_=th_col[:], func=ACT.Copy, scale=-1.0)

        a_banks = [ps.tile([P, BANK], F32, name="a_bank%d" % c) for c in range(CHUNKS)]
        ta_banks = [ps.tile([P, BANK], F32, name="ta_bank%d" % c) for c in range(CHUNKS)]
        a_sb = sb.tile([P, V], F32, name="a_sb")
        ta_sb = sb.tile([P, V], F32, name="ta_sb")
        chunk_max = column("chunk_max", CHUNKS)

        def copy_a(c):
            nc.vector.tensor_scalar(
                out=a_sb[:, cols(c)], in0=a_banks[c][:], scalar1=1.0, scalar2=None,
                op0=ALU.mult, op1=ALU.max, accum_out=chunk_max[:, c : c + 1],
            )

        for c in range(CHUNKS):
            scores(a_banks[c], c, hid_codes, hid_scales)
        for c in range(CHUNKS):
            copy_a(c)

        neg_max = column("neg_max")
        nc.vector.tensor_reduce(out=neg_max[:], in_=chunk_max[:], axis=AXIS.X, op=ALU.max, negate=True)
        dhid_codes, dhid_scales = quantise("dhid", dhid_grouped)
        for c in range(CHUNKS):
            scores(ta_banks[c], c, dhid_codes, dhid_scales)

        ax = sb.tile([P, SLOTS], F32, name="ax")
        nc.vector.tensor_copy(out=ax[:], in_=a_sb[:].indirect(offsets[:]))
        p = sb.tile([P, V], F32, name="p")
        z = column("z")
        nc.scalar.activation(out=p[:], in_=a_sb[:], func=ACT.Exp, bias=neg_max[:], accum_out=z[:])
        for c in (0, 1):
            nc.vector.tensor_copy(out=ta_sb[:, cols(c)], in_=ta_banks[c][:])

        turned = [(c, max(c * BANK, DIRECT), (c + 1) * BANK) for c in range(DIRECT // BANK, CHUNKS)]

        def turn(bank, source, lo, hi, start=False, stop=False):
            for at in range(lo, hi, P):
                nc.tensor.matmul(
                    out=bank[:, at % BANK : at % BANK + P],
                    lhsT=source[:, at : at + P],
                    rhs=identity[:],
                    is_transpose=True,
                    start=start and at == lo,
                    stop=stop and at == hi - P,
                )

        for c, lo, hi in turned:
            turn(a_banks[c], base_sb, lo, hi, start=True)

        def copy_ta_piece(c, lo, hi):
            nc.scalar.copy(out=ta_sb[:, c * BANK + lo * P : c * BANK + hi * P], in_=ta_banks[c][:, lo * P : hi * P])

        xp = sb.tile([P, V], F32, name="xp")
        xz_parts = column("xz_parts", 3)

        def make_xp(i, part, ta_part):
            nc.vector.scalar_tensor_tensor(
                out=xp[:, part], in0=ta_part, scalar=1.0, in1=p[:, part],
                op0=ALU.mult, op1=ALU.mult, accum_out=xz_parts[:, i : i + 1],
            )

        make_xp(0, cols(2), ta_banks[2][:])
        rz = column("rz")
        nc.vector.reciprocal(out=rz[:], in_=z[:])
        make_xp(1, slice(0, 2 * BANK), ta_sb[:, : 2 * BANK])

        neg_zt, e0, n0, n1, e1, n1m, n2, g1, g2, tanh_bias = (
            column(n) for n in ("neg_zt", "e0", "n0", "n1", "e1", "n1m", "n2", "g1", "g2", "tanh_bias")
        )
        copy_ta_piece(3, 0, 1)
        z_bits = z[:].bitcast(U32)
        nc.scalar.activation(out=e0[:], in_=z_bits, func=ACT.Exp, scale=-LOG_PER_BIT, bias=exp_bias[:])
        nc.scalar.activation(out=n0[:], in_=z_bits, func=ACT.Identity, scale=-0.5 * LOG_PER_BIT, bias=guess_bias[:])
        nc.scalar.activation(out=neg_zt[:], in_=z[:], func=ACT.Copy, scale=neg_th[:])
        copy_ta_piece(3, 1, 2)
        nc.scalar.activation(out=n1[:], in_=e0[:], func=ACT.Identity, scale=neg_zt[:], bias=n0[:])
        copy_ta_piece(3, 2, 4)
        nc.scalar.activation(out=e1[:], in_=n1[:], func=ACT.Exp, scale=2.0, bias=e1_const[:])
        nc.scalar.activation(out=n1m[:], in_=neg_max[:], func=ACT.Identity, scale=0.5, bias=n1[:])
        copy_ta_piece(2, 0, 2)
        nc.scalar.activation(out=g1[:], in_=e1[:], func=ACT.Square, scale=neg_zt[:], bias=square_const[:])
        nc.scalar.activation(out=n2[:], in_=e1[:], func=ACT.Identity, scale=neg_zt[:], bias=n1m[:])
        copy_ta_piece(2, 2, 3)
        nc.scalar.activation(out=g2[:], in_=g1[:], func=ACT.Square, scale=9.0 / LINEAR**2, bias=plus6[:])
        copy_ta_piece(2, 3, 4)
        nc.scalar.activation(out=tanh_bias[:], in_=g2[:], func=ACT.Identity, scale=1.0 / 648.0, bias=n2[:])
        t = sb.tile([P, SLOTS], F32, name="t")
        t2 = sb.tile([P, SLOTS], F32, name="t2")
        halves = (slice(0, SLOTS // 2), slice(SLOTS // 2, SLOTS))
        for half in halves:
            nc.scalar.activation(out=t[:, half], in_=ax[:, half], func=ACT.Tanh, scale=0.5, bias=tanh_bias[:])
        for half in halves:
            nc.scalar.activation(out=t2[:, half], in_=t[:, half], func=ACT.Square)

        make_xp(2, cols(3), ta_sb[:, cols(3)])
        rz_times = column("rz_times", 2)
        half_rz, minus2_rz = rz_times[:, 0:1], rz_times[:, 1:2]
        nc.scalar.activation(out=rz_times[:], in_=rz_factors[:], func=ACT.Copy, scale=rz[:])
        tx = sb.tile([P, SLOTS], F32, name="tx")
        nc.vector.tensor_copy(out=tx[:], in_=ta_sb[:].indirect(offsets[:]))
        xz, neg_mean = column("xz"), column("neg_mean")
        nc.gpsimd.tensor_scalar(
            out=xz[:], in0=xz_parts[:, 0:1], scalar1=xz_parts[:, 1:2], scalar2=xz_parts[:, 2:3], op0=ALU.add, op1=ALU.add
        )
        nc.gpsimd.tensor_scalar(out=neg_mean[:], in0=xz[:], scalar1=rz[:], scalar2=-1.0, op0=ALU.mult, op1=ALU.mult)

        h = sb.tile([P, SLOTS], F32, name="h")
        neg_w = sb.tile([P, SLOTS], F32, name="neg_w")
        xe1 = sb.tile([P, SLOTS], F32, name="xe1")
        neg_w_sum, xe1_sum = column("neg_w_sum"), column("xe1_sum")
        beta, neg_beta_mean, alpha = column("beta"), column("neg_beta_mean"), column("alpha")
        acc1 = sb.tile([P, DIRECT], F32, name="acc1")
        acc2 = sb.tile([P, DIRECT], F32, name="acc2")

        def add_xp(lo, hi):
            nc.vector.scalar_tensor_tensor(
                out=acc1[:, lo:hi], in0=xp[:, lo:hi], scalar=beta[:], in1=base_sb[:, lo:hi], op0=ALU.mult, op1=ALU.add
            )

        nc.vector.scalar_tensor_tensor(
            out=neg_w[:], in0=t2[:], scalar=-1.0, in1=sw_rows[:], op0=ALU.add, op1=ALU.mult,
            accum_out=neg_w_sum[:],
        )
        nc.scalar.activation(out=beta[:], in_=neg_w_sum[:], func=ACT.Copy, scale=half_rz)
        nc.vector.scalar_tensor_tensor(
            out=h[:], in0=tx[:], scalar=neg_mean[:], in1=t[:], op0=ALU.add, op1=ALU.mult
        )
        add_xp(0, 2 * P)
        nc.vector.scalar_tensor_tensor(
            out=xe1[:], in0=h[:], scalar=0.25, in1=neg_w[:], op0=ALU.mult, op1=ALU.mult,
            accum_out=xe1_sum[:],
        )
        add_xp(2 * P, DIRECT)
        nc.vector.tensor_copy(out=xs[:].indirect(offsets[:]), in_=xe1[:])

        xp_term = sb.tile([P, V], F32, name="xp_term")
        p_term = sb.tile([P, V], F32, name="p_term")
        turned_sum = sb.tile([P, V], F32, name="turned_sum")

        def scale_xp(c, lo, hi):
            nc.scalar.activation(out=xp_term[:, lo:hi], in_=xp[:, lo:hi], func=ACT.Copy, scale=beta[:])
            turn(a_banks[c], xp_term, lo, hi)

        def scale_p(c, lo, hi):
            nc.scalar.activation(out=p_term[:, lo:hi], in_=p[:, lo:hi], func=ACT.Copy, scale=alpha[:])
            turn(a_banks[c], p_term, lo, hi, stop=True)

        def turn_back(c, lo, hi):
            nc.scalar.copy(out=turned_sum[:, lo:hi], in_=a_banks[c][:, lo % BANK :])
            turn(ta_banks[c], turned_sum, lo, hi, start=True, stop=True)

        c, lo, hi = turned[0]
        scale_xp(c, lo, lo + P)
        scale_xp(c, lo + P, hi)
        nc.scalar.activation(out=neg_beta_mean[:], in_=beta[:], func=ACT.Copy, scale=neg_mean[:])
        c, lo, hi = turned[1]
        scale_xp(c, lo, lo + 2 * P)
        scale_xp(c, lo + 2 * P, hi)
        scale_xp(*turned[2])
        nc.gpsimd.tensor_scalar(
            out=alpha[:], in0=xe1_sum[:], scalar1=minus2_rz, scalar2=neg_beta_mean[:], op0=ALU.mult, op1=ALU.add
        )
        nc.gpsimd.tensor_scalar(
            out=p_term[:, :DIRECT], in0=p[:, :DIRECT], scalar1=alpha[:], scalar2=0.0, op0=ALU.mult, op1=ALU.add
        )
        nc.gpsimd.tensor_tensor(out=acc2[:], in0=acc1[:], in1=p_term[:, :DIRECT], op=ALU.add)
        for piece in turned:
            scale_p(*piece)
        for piece in turned:
            turn_back(*piece)

        result = sb.tile([P, V], F32, name="result")

        def finish(lo, hi, dense):
            nc.vector.scalar_tensor_tensor(
                out=result[:, lo:hi], in0=xs[:, lo:hi], scalar=2.0, in1=dense, op0=ALU.mult, op1=ALU.add
            )
            nc.sync.dma_start(out=out[:, lo:hi], in_=result[:, lo:hi])

        finish(0, DIRECT // 2, acc2[:, : DIRECT // 2])
        finish(DIRECT // 2, DIRECT, acc2[:, DIRECT // 2 :])
        c, lo, hi = turned[0]
        finish(lo, hi, ta_banks[c][:, lo % BANK :])
        c, lo, hi = turned[1]
        finish(lo, hi, ta_banks[c][:])
        c, lo, hi = turned[2]
        finish(lo, hi - LAST_STORE, ta_banks[c][:, : BANK - LAST_STORE])
        finish(hi - LAST_STORE, hi, ta_banks[c][:, BANK - LAST_STORE :])
